import numpy as np
import ml_dtypes


def mxq(x, axis, fmt="e4m3"):
    dtype, down = {"e4m3": (ml_dtypes.float8_e4m3fn, 7), "e5m2": (ml_dtypes.float8_e5m2, 14)}[fmt]
    v = np.moveaxis(np.asarray(x, np.float32).astype(ml_dtypes.bfloat16).astype(np.float64), axis, -1)
    blocks = v.reshape(v.shape[:-1] + (-1, 32))
    amax = np.abs(blocks).max(-1, keepdims=True)
    byte = np.maximum(np.where(amax > 0, np.frexp(amax)[1] - 1 + 127, 0) - down, 1)
    scale = np.exp2(byte - 127.0)
    codes = (blocks / scale).astype(np.float32).astype(dtype).astype(np.float64)
    return np.moveaxis((codes * scale).reshape(v.shape), -1, axis)


WIDE = False


def mx_kscale(k):
    if not WIDE:
        return np.ones(k)
    levels = np.array([10, -10, 5, -5, 0])
    if k % 512:
        return np.exp2(np.random.permutation(np.resize(levels, k // 32))).repeat(32)
    a = np.empty((k // 512, 16))
    for p in range(k // 512):
        a[p, :8] = np.random.permutation(np.resize(levels, 8))
        for g in range(8):
            far = levels[np.abs(levels - a[p, g]) >= 10]
            a[p, g + 8] = far[np.random.randint(len(far))]
    return np.exp2(a.ravel()).repeat(32)


def f64(x):
    return np.asarray(x).astype(np.float64)


def striped(idx):
    return np.tile(idx.reshape(-1, 16).T, (8, 1)).astype(np.uint16)


def unstriped(offs):
    return offs[:16].T.reshape(-1).astype(np.int64)


def pack_weight(w):
    k, n = w.shape
    w = f64(np.asarray(w, np.float32).astype(ml_dtypes.bfloat16)).reshape(k // 32, 32, n)
    amax = np.abs(w).max(1)
    byte = np.clip(np.where(amax > 0, np.frexp(amax)[1] - 1 + 127 - 7, 1), 1, 254)
    scaled = (w * np.exp2(127.0 - byte)[:, None, :]).reshape(k, n).astype(np.float32)
    words = np.ascontiguousarray(scaled.reshape(k // 512, 128, 4, n).transpose(0, 1, 3, 2)).astype(ml_dtypes.float8_e4m3fn).view(np.uint8)
    return words, np.ascontiguousarray(byte.astype(np.uint8).reshape(k // 512, 16, n))


def unpack_weight(words, scales):
    g, p, n, _ = words.shape
    vals = np.ascontiguousarray(words).view(ml_dtypes.float8_e4m3fn).astype(np.float64) * np.repeat(np.exp2(scales.astype(np.float64) - 127.0), 8, axis=1)[..., None]
    return vals.transpose(0, 1, 3, 2).reshape(g * 512, n)


def relu(v):
    return np.maximum(v, 0.0)


K, T, S, H, N, D = 1024, 2048, 512, 512, 256, 4


def setup_inputs():
    n = np.random.standard_normal
    s = mx_kscale(K)[:, None]
    u = mx_kscale(H)
    packed_xT = pack_weight(n((K, T)) * s)
    return {
        "x_words": packed_xT[0],
        "x_scales": packed_xT[1],
        "w1": (n((K, H)) / np.sqrt(K) / s * u).astype(np.float32),
        "w2": (n((H, N)) / np.sqrt(H) / u[:, None]).astype(np.float32),
        "w3": (n((H, N)) / np.sqrt(H) / u[:, None]).astype(np.float32),
        "offs": striped(np.random.permutation(T)[:S]),
    }


def reference(x_words, x_scales, w1, w2, w3, offs):
    xq = unpack_weight(x_words, x_scales)[:, unstriped(offs)]
    h = relu(mxq(f64(w1), 0, "e4m3").T @ xq)
    y = mxq(f64(w2), 0, "e4m3").T @ mxq(h, 0, "e4m3")
    z = h.reshape(len(h), -1, D).mean(axis=2)
    gg = mxq(f64(w3), 0, "e4m3").T @ mxq(z, 0, "e4m3")
    return relu(y + np.repeat(gg, D, axis=1))

@@ -1,0 +1,191 @@
+from contextlib import ExitStack
+
+import concourse.mybir as mybir
+
+K, T, S, H, N, D = 1024, 2048, 512, 512, 256, 4
+FLOPS = 2 * K * H * S + 2 * H * N * S + 2 * H * N * (S // D)
+
+F32 = mybir.dt.float32
+BF16 = mybir.dt.bfloat16
+I32 = mybir.dt.int32
+U32 = mybir.dt.uint32
+U16 = mybir.dt.uint16
+U8 = mybir.dt.uint8
+FP8X4 = mybir.dt.float8_e4m3fn_x4
+ACT = mybir.ActivationFunctionType
+ALU = mybir.AluOpType
+
+P = 128
+PACK = 4
+K_PASS = P * PACK
+PASSES = K // K_PASS
+HALVES = 2
+HALF = S // HALVES
+CHUNK = 128
+CLOUDS = HALF // D
+M_TILES = N // P
+
+
+def tile_picked_ypnseg_mean_p_kernel(tc, x_words, x_scales, w1, w2, w3, offs, out):
+    nc = tc.nc
+    with ExitStack() as ctx:
+        keep = ctx.enter_context(tc.tile_pool(name="keep", bufs=1))
+        psum = ctx.enter_context(tc.psum_pool(name="psum", bufs=1))
+
+        def sb(name, shape, dtype):
+            return keep.tile(shape, dtype, name=name, align_bytes=64)
+
+        offsets = keep.tile([P, S // 16], U16, name="offsets")
+        nc.sync.dma_start(offsets[:], offs)
+
+        def load_rows(name, rows):
+            raw = sb(name, [P, PACK, rows.shape[1]], F32)
+            nc.sync.dma_start(out=raw[:], in_=rows.rearrange("(p j) c -> p j c", j=PACK))
+            return raw
+
+        def load_words(o):
+            words = sb("x_words%d" % o, [P, T], U32)
+            nc.sync.dma_start(out=words[:].bitcast(I32), in_=x_words[o].rearrange("p n t -> p (n t)").bitcast(I32))
+            return words
+
+        x_planes = sb("x_planes", [P, T], U8)
+        nc.vector.memset(x_planes[:].bitcast(I32), 0)
+        w1_raw = [load_rows("w1_raw0", w1[0:K_PASS, :])]
+        for q in range(4):
+            nc.scalar.dma_start(
+                out=x_planes[32 * q : 32 * q + 4 * PASSES, :].bitcast(I32),
+                in_=x_scales[:, 4 * q : 4 * q + 4, :].bitcast(I32),
+            )
+        w1_raw.append(load_rows("w1_raw1", w1[K_PASS:K, :]))
+        w2_raw = load_rows("w2_raw", w2)
+        x_sb = [load_words(o) for o in range(PASSES)]
+        w3_raw = load_rows("w3_raw", w3)
+
+        def quantise(name, values, width):
+            codes = sb(name + "_codes", [P, width], U32)
+            scales = sb(name + "_scales", [P, width], U8)
+            nc.vector.quantize_mx(out=codes[:].bitcast(FP8X4), scales=scales[:], in_=values)
+            return codes, scales
+
+        picked_planes = sb("picked_planes", [P, S], U8)
+        nc.vector.tensor_copy(picked_planes[:], x_planes[:].indirect(offsets[:]))
+
+        w1_q = []
+        for o in range(PASSES):
+            src = w1_raw[o][:].rearrange("p j (m t) -> p m j t", t=PACK)
+            both = []
+            for u in range(2):
+                grouped = sb("w1_bf%d_%d" % (o, u), [P, 2 * P * PACK], BF16)
+                dst = grouped[:].rearrange("p (t m j) -> p m j t", t=2, j=PACK)
+                if u == 0:
+                    nc.vector.tensor_copy(out=dst, in_=src[:, :, :, 0:2])
+                else:
+                    nc.scalar.activation(out=dst, in_=src[:, :, :, 2:4], func=ACT.Copy)
+                both.append(quantise("w1_%d_%d" % (o, u), grouped[:], 2 * P))
+            w1_q.append(both)
+
+        def group_views(name, raw):
+            grouped = sb(name, [P, N * PACK], BF16)
+            dst = grouped[:].rearrange("p (c i j) -> p c j i", i=4, j=PACK)
+            src = raw[:].rearrange("p j (c i) -> p c j i", i=4)
+            return grouped, dst, src
+
+        w2_bf, dst, src = group_views("w2_bf", w2_raw)
+        nc.scalar.activation(out=dst, in_=src, func=ACT.Copy)
+        w2_codes, w2_scales = quantise("w2", w2_bf[:], N)
+
+        h_banks = [psum.tile([P, PACK, CHUNK], F32, name="h_bank%d" % c) for c in range(S // CHUNK)]
+        for o in range(PASSES):
+            for half in range(HALVES):
+                picked = sb("picked%d_%d" % (o, half), [P, HALF], U32)
+                cols = HALF // 16
+                nc.vector.tensor_copy(picked[:], x_sb[o][:].indirect(offsets[:, half * cols : (half + 1) * cols]))
+                for cc in range(HALF // CHUNK):
+                    c = half * (HALF // CHUNK) + cc
+                    for t in range(PACK):
+                        codes, scales = w1_q[o][t // 2]
+                        tc_cols = slice((t % 2) * P, (t % 2 + 1) * P)
+                        nc.tensor.matmul_mx(
+                            out=h_banks[c][:, t, :],
+                            lhsT=codes[:, tc_cols].bitcast(FP8X4),
+                            lhsT_scale=scales[:, tc_cols],
+                            rhs=picked[:, cc * CHUNK : (cc + 1) * CHUNK].bitcast(FP8X4),
+                            rhs_scale=picked_planes[4 * o : P, c * CHUNK : (c + 1) * CHUNK],
+                            start=(o == 0 and t == 0),
+                            stop=(o == PASSES - 1 and t == PACK - 1),
+                        )
+
+        w3_bf, dst, src = group_views("w3_bf", w3_raw)
+        nc.vector.tensor_copy(out=dst, in_=src)
+        w3_codes, w3_scales = quantise("w3", w3_bf[:], N)
+
+        quarter = []
+        h_bf = []
+        per = CHUNK // D
+        for half in range(HALVES):
+            quarter.append(sb("quarter%d" % half, [P, D, CLOUDS, PACK], F32))
+            h_bf.append(sb("h_bf%d" % half, [P, D, CLOUDS, PACK], BF16))
+            for cc in range(HALF // CHUNK):
+                bank = h_banks[half * (HALF // CHUNK) + cc]
+                nc.scalar.activation(
+                    out=quarter[half][:, :, cc * per : (cc + 1) * per, :],
+                    in_=bank[:].rearrange("p t (v d) -> p d v t", d=D),
+                    func=ACT.Relu,
+                    scale=1.0 / D,
+                )
+        for cc in range(HALF // CHUNK):
+            bank = h_banks[(HALF // CHUNK) + cc]
+            nc.scalar.activation(
+                out=h_bf[1][:, :, cc * per : (cc + 1) * per, :],
+                in_=bank[:].rearrange("p t (v d) -> p d v t", d=D),
+                func=ACT.Relu,
+            )
+
+        for half in range(HALVES):
+            flat = quarter[half][:].rearrange("p d v t -> p (d v t)")
+            row = CLOUDS * PACK
+            pairs = sb("pairs%d" % half, [P, 2 * row], F32)
+            nc.vector.tensor_tensor(out=pairs[:], in0=flat[:, 0 : 2 * row], in1=flat[:, 2 * row : 4 * row], op=ALU.add)
+            h_flat = h_bf[half][:].rearrange("p d v t -> p (d v t)")
+            if half == 0:
+                nc.vector.tensor_scalar(out=h_flat, in0=flat, scalar1=float(D), scalar2=None, op0=ALU.mult)
+            z_bf = sb("z_bf%d" % half, [P, row], BF16)
+            nc.vector.tensor_tensor(out=z_bf[:], in0=pairs[:, 0:row], in1=pairs[:, row : 2 * row], op=ALU.add)
+            h_codes, h_scales = quantise("h%d" % half, h_flat, HALF)
+            z_codes = sb("z_codes%d" % half, [P, 2 * CLOUDS], U32)
+            z_scales = sb("z_scales%d" % half, [P, 2 * CLOUDS], U8)
+            for e in range(2):
+                cl = slice(e * CLOUDS, (e + 1) * CLOUDS)
+                nc.vector.quantize_mx(out=z_codes[:, cl].bitcast(FP8X4), scales=z_scales[:, cl], in_=z_bf[:])
+
+            for m in range(M_TILES):
+                mc = slice(m * P, (m + 1) * P)
+                acc = psum.tile([P, HALF], F32, name="acc%d_%d" % (half, m))
+                nc.tensor.matmul_mx(
+                    out=acc[:],
+                    lhsT=w2_codes[:, mc].bitcast(FP8X4),
+                    lhsT_scale=w2_scales[:, mc],
+                    rhs=h_codes[:].bitcast(FP8X4),
+                    rhs_scale=h_scales[:],
+                    start=True,
+                    stop=False,
+                )
+                for e in range(2):
+                    nc.tensor.matmul_mx(
+                        out=acc[:, e * P : (e + 1) * P],
+                        lhsT=w3_codes[:, mc].bitcast(FP8X4),
+                        lhsT_scale=w3_scales[:, mc],
+                        rhs=z_codes[:].bitcast(FP8X4),
+                        rhs_scale=z_scales[:],
+                        start=False,
+                        stop=(e == 1),
+                    )
+                result = sb("result%d_%d" % (half, m), [P, CLOUDS, D], F32)
+                ordered = acc[:].rearrange("p (d v) -> p v d", d=D)
+                if half == HALVES - 1 and m == M_TILES - 1:
+                    nc.vector.tensor_scalar(out=result[:], in0=ordered, scalar1=0.0, scalar2=None, op0=ALU.max)
+                else:
+                    nc.scalar.activation(out=result[:], in_=ordered, func=ACT.Relu)
+                nc.sync.dma_start(
+                    out=out[mc, half * HALF : (half + 1) * HALF], in_=result[:].rearrange("p v d -> p (v d)")
+                )

@@ -38,9 +38,12 @@ def tile_picked_ypnseg_mean_p_kernel(tc, x_words, x_scales, w1, w2, w3, offs, ou
         offsets = keep.tile([P, S // 16], U16, name="offsets")
         nc.sync.dma_start(offsets[:], offs)
 
-        def load_rows(name, rows):
+        def load_rows(name, rows, pieces):
             raw = sb(name, [P, PACK, rows.shape[1]], F32)
-            nc.sync.dma_start(out=raw[:], in_=rows.rearrange("(p j) c -> p j c", j=PACK))
+            view = rows.rearrange("(p j) c -> p j c", j=PACK)
+            step = PACK // pieces
+            for j in range(0, PACK, step):
+                nc.sync.dma_start(out=raw[:, j : j + step, :], in_=view[:, j : j + step, :])
             return raw
 
         def load_words(o):
@@ -50,16 +53,16 @@ def tile_picked_ypnseg_mean_p_kernel(tc, x_words, x_scales, w1, w2, w3, offs, ou
 
         x_planes = sb("x_planes", [P, T], U8)
         nc.vector.memset(x_planes[:].bitcast(I32), 0)
-        w1_raw = [load_rows("w1_raw0", w1[0:K_PASS, :])]
+        w1_raw = [load_rows("w1_raw0", w1[0:K_PASS, :], 2)]
         for q in range(4):
-            nc.scalar.dma_start(
+            nc.sync.dma_start(
                 out=x_planes[32 * q : 32 * q + 4 * PASSES, :].bitcast(I32),
                 in_=x_scales[:, 4 * q : 4 * q + 4, :].bitcast(I32),
             )
-        w1_raw.append(load_rows("w1_raw1", w1[K_PASS:K, :]))
-        w2_raw = load_rows("w2_raw", w2)
+        w1_raw.append(load_rows("w1_raw1", w1[K_PASS:K, :], 2))
+        w2_raw = load_rows("w2_raw", w2, 1)
         x_sb = [load_words(o) for o in range(PASSES)]
-        w3_raw = load_rows("w3_raw", w3)
+        w3_raw = load_rows("w3_raw", w3, 1)
 
         def quantise(name, values, width):
             codes = sb(name + "_codes", [P, width], U32)
@@ -149,9 +152,12 @@ def tile_picked_ypnseg_mean_p_kernel(tc, x_words, x_scales, w1, w2, w3, offs, ou
             h_flat = h_bf[half][:].rearrange("p d v t -> p (d v t)")
             if half == 0:
                 nc.vector.tensor_scalar(out=h_flat, in0=flat, scalar1=float(D), scalar2=None, op0=ALU.mult)
+            else:
+                h_codes, h_scales = quantise("h%d" % half, h_flat, HALF)
             z_bf = sb("z_bf%d" % half, [P, row], BF16)
             nc.vector.tensor_tensor(out=z_bf[:], in0=pairs[:, 0:row], in1=pairs[:, row : 2 * row], op=ALU.add)
-            h_codes, h_scales = quantise("h%d" % half, h_flat, HALF)
+            if half == 0:
+                h_codes, h_scales = quantise("h%d" % half, h_flat, HALF)
             z_codes = sb("z_codes%d" % half, [P, 2 * CLOUDS], U32)
             z_scales = sb("z_scales%d" % half, [P, 2 * CLOUDS], U8)
             for e in range(2):

@@ -38,12 +38,9 @@ def tile_picked_ypnseg_mean_p_kernel(tc, x_words, x_scales, w1, w2, w3, offs, ou
         offsets = keep.tile([P, S // 16], U16, name="offsets")
         nc.sync.dma_start(offsets[:], offs)
 
-        def load_rows(name, rows, pieces):
-            raw = sb(name, [P, PACK, rows.shape[1]], F32)
-            view = rows.rearrange("(p j) c -> p j c", j=PACK)
-            step = PACK // pieces
-            for j in range(0, PACK, step):
-                nc.sync.dma_start(out=raw[:, j : j + step, :], in_=view[:, j : j + step, :])
+        def load_rows(name, rows, tag):
+            raw = keep.tile([P, PACK, rows.shape[1]], F32, name=name, tag=tag, align_bytes=64)
+            nc.sync.dma_start(out=raw[:], in_=rows.rearrange("(p j) c -> p j c", j=PACK))
             return raw
 
         def load_words(o):
@@ -51,27 +48,32 @@ def tile_picked_ypnseg_mean_p_kernel(tc, x_words, x_scales, w1, w2, w3, offs, ou
             nc.sync.dma_start(out=words[:].bitcast(I32), in_=x_words[o].rearrange("p n t -> p (n t)").bitcast(I32))
             return words
 
-        x_planes = sb("x_planes", [P, T], U8)
-        nc.vector.memset(x_planes[:].bitcast(I32), 0)
-        w1_raw = [load_rows("w1_raw0", w1[0:K_PASS, :], 2)]
+        scale_rows = sb("scale_rows", [P, T], U8)
+        nc.sync.dma_start(
+            out=scale_rows[0:32, :].bitcast(I32), in_=x_scales.rearrange("o r n -> r o n").bitcast(I32)
+        )
+        nc.vector.memset(scale_rows[32:64, :].bitcast(I32), 0)
+        nc.vector.memset(scale_rows[64:P, :].bitcast(I32), 0)
+        picked_planes = sb("picked_planes", [P, PASSES, S], U8)
+        nc.vector.memset(picked_planes[:].rearrange("p o s -> p (o s)").bitcast(I32), 0)
+        w1_raw = [load_rows("w1_raw%d" % o, w1[o * K_PASS : (o + 1) * K_PASS, :], "w1_raw%d" % o) for o in range(PASSES)]
+        x_sb = [load_words(0)]
+        w2_raw = load_rows("w2_raw", w2, "w2_raw")
+        x_sb.append(load_words(1))
+
+        picked_rows = sb("picked_rows", [P, S], U8)
+        nc.vector.tensor_copy(picked_rows[:], scale_rows[:].indirect(offsets[:]))
         for q in range(4):
-            nc.sync.dma_start(
-                out=x_planes[32 * q : 32 * q + 4 * PASSES, :].bitcast(I32),
-                in_=x_scales[:, 4 * q : 4 * q + 4, :].bitcast(I32),
+            nc.scalar.dma_start(
+                out=picked_planes[32 * q : 32 * q + 4].rearrange("p o s -> p (o s)").bitcast(I32),
+                in_=picked_rows[8 * q : 8 * q + 8, :].bitcast(I32),
             )
-        w1_raw.append(load_rows("w1_raw1", w1[K_PASS:K, :], 2))
-        w2_raw = load_rows("w2_raw", w2, 1)
-        x_sb = [load_words(o) for o in range(PASSES)]
-        w3_raw = load_rows("w3_raw", w3, 1)
 
         def quantise(name, values, width):
             codes = sb(name + "_codes", [P, width], U32)
             scales = sb(name + "_scales", [P, width], U8)
             nc.vector.quantize_mx(out=codes[:].bitcast(FP8X4), scales=scales[:], in_=values)
             return codes, scales
-
-        picked_planes = sb("picked_planes", [P, S], U8)
-        nc.vector.tensor_copy(picked_planes[:], x_planes[:].indirect(offsets[:]))
 
         w1_q = []
         for o in range(PASSES):
@@ -86,6 +88,8 @@ def tile_picked_ypnseg_mean_p_kernel(tc, x_words, x_scales, w1, w2, w3, offs, ou
                     nc.scalar.activation(out=dst, in_=src[:, :, :, 2:4], func=ACT.Copy)
                 both.append(quantise("w1_%d_%d" % (o, u), grouped[:], 2 * P))
             w1_q.append(both)
+
+        w3_raw = load_rows("w3_raw", w3, "w1_raw0")
 
         def group_views(name, raw):
             grouped = sb(name, [P, N * PACK], BF16)
@@ -113,85 +117,126 @@ def tile_picked_ypnseg_mean_p_kernel(tc, x_words, x_scales, w1, w2, w3, offs, ou
                             lhsT=codes[:, tc_cols].bitcast(FP8X4),
                             lhsT_scale=scales[:, tc_cols],
                             rhs=picked[:, cc * CHUNK : (cc + 1) * CHUNK].bitcast(FP8X4),
-                            rhs_scale=picked_planes[4 * o : P, c * CHUNK : (c + 1) * CHUNK],
+                            rhs_scale=picked_planes[:, o, c * CHUNK : (c + 1) * CHUNK],
                             start=(o == 0 and t == 0),
                             stop=(o == PASSES - 1 and t == PACK - 1),
                         )
 
-        w3_bf, dst, src = group_views("w3_bf", w3_raw)
-        nc.vector.tensor_copy(out=dst, in_=src)
-        w3_codes, w3_scales = quantise("w3", w3_bf[:], N)
-
-        quarter = []
-        h_bf = []
         per = CHUNK // D
+        banks_a_half = HALF // CHUNK
+        even, pairs, h_bf, z_bf = [], [], [], []
         for half in range(HALVES):
-            quarter.append(sb("quarter%d" % half, [P, D, CLOUDS, PACK], F32))
+            even.append(sb("even%d" % half, [P, HALF // 2, PACK], F32))
+            pairs.append(sb("pairs%d" % half, [P, HALF // 2, PACK], F32))
             h_bf.append(sb("h_bf%d" % half, [P, D, CLOUDS, PACK], BF16))
-            for cc in range(HALF // CHUNK):
-                bank = h_banks[half * (HALF // CHUNK) + cc]
+            z_bf.append(sb("z_bf%d" % half, [P, CLOUDS, PACK], BF16))
+
+        def banks_of(half):
+            return enumerate(h_banks[half * banks_a_half : (half + 1) * banks_a_half])
+
+        def read_even(half):
+            for cc, bank in banks_of(half):
+                ss = slice(cc * CHUNK // 2, (cc + 1) * CHUNK // 2)
+                by_parity = bank[:].rearrange("p t (s e) -> p e s t", e=2)
+                nc.scalar.activation(out=even[half][:, ss, :], in_=by_parity[:, 0], func=ACT.Relu)
+
+        def add_odd(half):
+            for cc, bank in banks_of(half):
+                ss = slice(cc * CHUNK // 2, (cc + 1) * CHUNK // 2)
+                by_parity = bank[:].rearrange("p t (s e) -> p e s t", e=2)
+                nc.vector.scalar_tensor_tensor(
+                    out=pairs[half][:, ss, :],
+                    in0=by_parity[:, 1],
+                    scalar=0.0,
+                    in1=even[half][:, ss, :],
+                    op0=ALU.max,
+                    op1=ALU.add,
+                )
+
+        def round_odd(half):
+            h_rows = h_bf[half][:].rearrange("p (f e) v t -> p e f v t", e=2)
+            for cc, bank in banks_of(half):
+                odd = bank[:].rearrange("p t (v f e) -> p e f v t", f=2, e=2)[:, 1]
+                nc.scalar.activation(out=h_rows[:, 1, :, cc * per : (cc + 1) * per, :], in_=odd, func=ACT.Relu)
+
+        def round_even(half):
+            h_rows = h_bf[half][:].rearrange("p (f e) v t -> p e f v t", e=2)
+            nc.vector.tensor_copy(out=h_rows[:, 0], in_=even[half][:].rearrange("p (v f) t -> p f v t", f=2))
+
+        def round_all(half):
+            for cc, bank in banks_of(half):
                 nc.scalar.activation(
-                    out=quarter[half][:, :, cc * per : (cc + 1) * per, :],
+                    out=h_bf[half][:, :, cc * per : (cc + 1) * per, :],
                     in_=bank[:].rearrange("p t (v d) -> p d v t", d=D),
                     func=ACT.Relu,
-                    scale=1.0 / D,
                 )
-        for cc in range(HALF // CHUNK):
-            bank = h_banks[(HALF // CHUNK) + cc]
-            nc.scalar.activation(
-                out=h_bf[1][:, :, cc * per : (cc + 1) * per, :],
-                in_=bank[:].rearrange("p t (v d) -> p d v t", d=D),
-                func=ACT.Relu,
-            )
 
-        for half in range(HALVES):
-            flat = quarter[half][:].rearrange("p d v t -> p (d v t)")
-            row = CLOUDS * PACK
-            pairs = sb("pairs%d" % half, [P, 2 * row], F32)
-            nc.vector.tensor_tensor(out=pairs[:], in0=flat[:, 0 : 2 * row], in1=flat[:, 2 * row : 4 * row], op=ALU.add)
-            h_flat = h_bf[half][:].rearrange("p d v t -> p (d v t)")
-            if half == 0:
-                nc.vector.tensor_scalar(out=h_flat, in0=flat, scalar1=float(D), scalar2=None, op0=ALU.mult)
-            else:
-                h_codes, h_scales = quantise("h%d" % half, h_flat, HALF)
-            z_bf = sb("z_bf%d" % half, [P, row], BF16)
-            nc.vector.tensor_tensor(out=z_bf[:], in0=pairs[:, 0:row], in1=pairs[:, row : 2 * row], op=ALU.add)
-            if half == 0:
-                h_codes, h_scales = quantise("h%d" % half, h_flat, HALF)
+        def pool(half):
+            by_cloud = pairs[half][:].rearrange("p (v f) t -> p f v t", f=2)
+            nc.vector.tensor_tensor(out=z_bf[half][:], in0=by_cloud[:, 0], in1=by_cloud[:, 1], op=ALU.add)
+
+        def quantise_h(half):
+            return quantise("h%d" % half, h_bf[half][:].rearrange("p d v t -> p (d v t)"), HALF)
+
+        def quantise_z(half):
             z_codes = sb("z_codes%d" % half, [P, 2 * CLOUDS], U32)
             z_scales = sb("z_scales%d" % half, [P, 2 * CLOUDS], U8)
             for e in range(2):
                 cl = slice(e * CLOUDS, (e + 1) * CLOUDS)
-                nc.vector.quantize_mx(out=z_codes[:, cl].bitcast(FP8X4), scales=z_scales[:, cl], in_=z_bf[:])
-
-            for m in range(M_TILES):
-                mc = slice(m * P, (m + 1) * P)
-                acc = psum.tile([P, HALF], F32, name="acc%d_%d" % (half, m))
-                nc.tensor.matmul_mx(
-                    out=acc[:],
-                    lhsT=w2_codes[:, mc].bitcast(FP8X4),
-                    lhsT_scale=w2_scales[:, mc],
-                    rhs=h_codes[:].bitcast(FP8X4),
-                    rhs_scale=h_scales[:],
-                    start=True,
-                    stop=False,
+                nc.vector.quantize_mx(
+                    out=z_codes[:, cl].bitcast(FP8X4),
+                    scales=z_scales[:, cl],
+                    in_=z_bf[half][:].rearrange("p v t -> p (v t)"),
                 )
+            return z_codes, z_scales
+
+        def product(acc, weights, m, values, start, stop):
+            mc = slice(m * P, (m + 1) * P)
+            nc.tensor.matmul_mx(
+                out=acc,
+                lhsT=weights[0][:, mc].bitcast(FP8X4),
+                lhsT_scale=weights[1][:, mc],
+                rhs=values[0][:].bitcast(FP8X4),
+                rhs_scale=values[1][:],
+                start=start,
+                stop=stop,
+            )
+
+        def head(half, h_q, z_q, y_first, on_vector):
+            for m in range(M_TILES):
+                acc = psum.tile([P, HALF], F32, name="acc%d_%d" % (half, m))
+                if y_first:
+                    product(acc[:], w2_q, m, h_q, True, False)
                 for e in range(2):
-                    nc.tensor.matmul_mx(
-                        out=acc[:, e * P : (e + 1) * P],
-                        lhsT=w3_codes[:, mc].bitcast(FP8X4),
-                        lhsT_scale=w3_scales[:, mc],
-                        rhs=z_codes[:].bitcast(FP8X4),
-                        rhs_scale=z_scales[:],
-                        start=False,
-                        stop=(e == 1),
-                    )
+                    product(acc[:, e * P : (e + 1) * P], w3_q, m, z_q, e == 0 and not y_first, e == 1 and y_first)
+                if not y_first:
+                    product(acc[:], w2_q, m, h_q, False, True)
                 result = sb("result%d_%d" % (half, m), [P, CLOUDS, D], F32)
                 ordered = acc[:].rearrange("p (d v) -> p v d", d=D)
-                if half == HALVES - 1 and m == M_TILES - 1:
+                if m in on_vector:
                     nc.vector.tensor_scalar(out=result[:], in0=ordered, scalar1=0.0, scalar2=None, op0=ALU.max)
                 else:
                     nc.scalar.activation(out=result[:], in_=ordered, func=ACT.Relu)
                 nc.sync.dma_start(
-                    out=out[mc, half * HALF : (half + 1) * HALF], in_=result[:].rearrange("p v d -> p (v d)")
+                    out=out[m * P : (m + 1) * P, half * HALF : (half + 1) * HALF],
+                    in_=result[:].rearrange("p v d -> p (v d)"),
                 )
+
+        w2_q = (w2_codes, w2_scales)
+        w3_bf, dst, src = group_views("w3_bf", w3_raw)
+        nc.vector.tensor_scalar(out=dst, in0=src, scalar1=1.0 / D, scalar2=None, op0=ALU.mult)
+        read_even(0)
+        read_even(1)
+        add_odd(0)
+        add_odd(1)
+        round_all(0)
+        round_all(1)
+        pool(0)
+        w3_q = quantise("w3", w3_bf[:], N)
+        z_q0 = quantise_z(0)
+        h_q0 = quantise_h(0)
+        pool(1)
+        head(0, h_q0, z_q0, False, ())
+        z_q1 = quantise_z(1)
+        h_q1 = quantise_h(1)
+        head(1, h_q1, z_q1, False, (1,))

@@ -43,11 +43,6 @@ def tile_picked_ypnseg_mean_p_kernel(tc, x_words, x_scales, w1, w2, w3, offs, ou
             nc.sync.dma_start(out=raw[:], in_=rows.rearrange("(p j) c -> p j c", j=PACK))
             return raw
 
-        def load_words(o):
-            words = sb("x_words%d" % o, [P, T], U32)
-            nc.sync.dma_start(out=words[:].bitcast(I32), in_=x_words[o].rearrange("p n t -> p (n t)").bitcast(I32))
-            return words
-
         scale_rows = sb("scale_rows", [P, T], U8)
         nc.sync.dma_start(
             out=scale_rows[0:32, :].bitcast(I32), in_=x_scales.rearrange("o r n -> r o n").bitcast(I32)
@@ -57,17 +52,18 @@ def tile_picked_ypnseg_mean_p_kernel(tc, x_words, x_scales, w1, w2, w3, offs, ou
         picked_planes = sb("picked_planes", [P, PASSES, S], U8)
         nc.vector.memset(picked_planes[:].rearrange("p o s -> p (o s)").bitcast(I32), 0)
         w1_raw = [load_rows("w1_raw%d" % o, w1[o * K_PASS : (o + 1) * K_PASS, :], "w1_raw%d" % o) for o in range(PASSES)]
-        x_sb = [load_words(0)]
-        w2_raw = load_rows("w2_raw", w2, "w2_raw")
-        x_sb.append(load_words(1))
 
         picked_rows = sb("picked_rows", [P, S], U8)
         nc.vector.tensor_copy(picked_rows[:], scale_rows[:].indirect(offsets[:]))
         for q in range(4):
-            nc.scalar.dma_start(
+            nc.sync.dma_start(
                 out=picked_planes[32 * q : 32 * q + 4].rearrange("p o s -> p (o s)").bitcast(I32),
                 in_=picked_rows[8 * q : 8 * q + 8, :].bitcast(I32),
             )
+
+        x_sb = keep.tile([P, PASSES, T], U32, name="x_sb", tag="scale_rows", align_bytes=64)
+        for o in range(PASSES):
+            nc.sync.dma_start(out=x_sb[:, o, :].bitcast(I32), in_=x_words[o].rearrange("p n t -> p (n t)").bitcast(I32))
 
         def quantise(name, values, width):
             codes = sb(name + "_codes", [P, width], U32)
@@ -90,6 +86,7 @@ def tile_picked_ypnseg_mean_p_kernel(tc, x_words, x_scales, w1, w2, w3, offs, ou
             w1_q.append(both)
 
         w3_raw = load_rows("w3_raw", w3, "w1_raw0")
+        w2_raw = load_rows("w2_raw", w2, "w1_raw1")
 
         def group_views(name, raw):
             grouped = sb(name, [P, N * PACK], BF16)
@@ -97,16 +94,12 @@ def tile_picked_ypnseg_mean_p_kernel(tc, x_words, x_scales, w1, w2, w3, offs, ou
             src = raw[:].rearrange("p j (c i) -> p c j i", i=4)
             return grouped, dst, src
 
-        w2_bf, dst, src = group_views("w2_bf", w2_raw)
-        nc.scalar.activation(out=dst, in_=src, func=ACT.Copy)
-        w2_codes, w2_scales = quantise("w2", w2_bf[:], N)
-
         h_banks = [psum.tile([P, PACK, CHUNK], F32, name="h_bank%d" % c) for c in range(S // CHUNK)]
         for o in range(PASSES):
             for half in range(HALVES):
                 picked = sb("picked%d_%d" % (o, half), [P, HALF], U32)
                 cols = HALF // 16
-                nc.vector.tensor_copy(picked[:], x_sb[o][:].indirect(offsets[:, half * cols : (half + 1) * cols]))
+                nc.vector.tensor_copy(picked[:], x_sb[:, o, :].indirect(offsets[:, half * cols : (half + 1) * cols]))
                 for cc in range(HALF // CHUNK):
                     c = half * (HALF // CHUNK) + cc
                     for t in range(PACK):
@@ -124,10 +117,11 @@ def tile_picked_ypnseg_mean_p_kernel(tc, x_words, x_scales, w1, w2, w3, offs, ou
 
         per = CHUNK // D
         banks_a_half = HALF // CHUNK
+        all_pairs = keep.tile([P, HALVES, HALF // 2, PACK], F32, name="pairs", align_bytes=64)
         even, pairs, h_bf, z_bf = [], [], [], []
         for half in range(HALVES):
             even.append(sb("even%d" % half, [P, HALF // 2, PACK], F32))
-            pairs.append(sb("pairs%d" % half, [P, HALF // 2, PACK], F32))
+            pairs.append(all_pairs[:, half])
             h_bf.append(sb("h_bf%d" % half, [P, D, CLOUDS, PACK], BF16))
             z_bf.append(sb("z_bf%d" % half, [P, CLOUDS, PACK], BF16))
 
@@ -140,8 +134,8 @@ def tile_picked_ypnseg_mean_p_kernel(tc, x_words, x_scales, w1, w2, w3, offs, ou
                 by_parity = bank[:].rearrange("p t (s e) -> p e s t", e=2)
                 nc.scalar.activation(out=even[half][:, ss, :], in_=by_parity[:, 0], func=ACT.Relu)
 
-        def add_odd(half):
-            for cc, bank in banks_of(half):
+        def add_odd(half, cc):
+            for bank in h_banks[half * banks_a_half + cc : half * banks_a_half + cc + 1]:
                 ss = slice(cc * CHUNK // 2, (cc + 1) * CHUNK // 2)
                 by_parity = bank[:].rearrange("p t (s e) -> p e s t", e=2)
                 nc.vector.scalar_tensor_tensor(
@@ -171,8 +165,20 @@ def tile_picked_ypnseg_mean_p_kernel(tc, x_words, x_scales, w1, w2, w3, offs, ou
                     func=ACT.Relu,
                 )
 
+        def round_rows(half, cc, rows):
+            bank = h_banks[half * banks_a_half + cc]
+            nc.scalar.activation(
+                out=h_bf[half][:, rows, cc * per : (cc + 1) * per, :],
+                in_=bank[:].rearrange("p t (v d) -> p d v t", d=D)[:, rows],
+                func=ACT.Relu,
+            )
+
+        def quantise_rows(half, e):
+            rows = h_bf[half][:, 2 * e : 2 * e + 2].rearrange("p d v t -> p (d v t)")
+            return quantise("h%d_%d" % (half, e), rows, P)
+
         def pool(half):
-            by_cloud = pairs[half][:].rearrange("p (v f) t -> p f v t", f=2)
+            by_cloud = pairs[half].rearrange("p (v f) t -> p f v t", f=2)
             nc.vector.tensor_tensor(out=z_bf[half][:], in0=by_cloud[:, 0], in1=by_cloud[:, 1], op=ALU.add)
 
         def quantise_h(half):
@@ -202,41 +208,50 @@ def tile_picked_ypnseg_mean_p_kernel(tc, x_words, x_scales, w1, w2, w3, offs, ou
                 stop=stop,
             )
 
-        def head(half, h_q, z_q, y_first, on_vector):
-            for m in range(M_TILES):
-                acc = psum.tile([P, HALF], F32, name="acc%d_%d" % (half, m))
-                if y_first:
-                    product(acc[:], w2_q, m, h_q, True, False)
+        def head(half, h_q, z_q, on_vector):
+            accs = [psum.tile([P, HALF], F32, name="acc%d_%d" % (half, m), tag="acc%d_%d" % (half, m)) for m in range(M_TILES)]
+            for m, acc in enumerate(accs):
                 for e in range(2):
-                    product(acc[:, e * P : (e + 1) * P], w3_q, m, z_q, e == 0 and not y_first, e == 1 and y_first)
-                if not y_first:
-                    product(acc[:], w2_q, m, h_q, False, True)
+                    product(acc[:, e * P : (e + 1) * P], w3_q, m, z_q, e == 0, False)
+            width = HALF // len(h_q)
+            for e, piece in enumerate(h_q[:-1]):
+                for m, acc in enumerate(accs):
+                    product(acc[:, e * width : (e + 1) * width], w2_q, m, piece, False, False)
+            for m, acc in enumerate(accs):
+                product(acc[:, HALF - width :], w2_q, m, h_q[-1], False, True)
                 result = sb("result%d_%d" % (half, m), [P, CLOUDS, D], F32)
                 ordered = acc[:].rearrange("p (d v) -> p v d", d=D)
                 if m in on_vector:
                     nc.vector.tensor_scalar(out=result[:], in0=ordered, scalar1=0.0, scalar2=None, op0=ALU.max)
                 else:
                     nc.scalar.activation(out=result[:], in_=ordered, func=ACT.Relu)
-                nc.sync.dma_start(
+                queue = nc.sync
+                queue.dma_start(
                     out=out[m * P : (m + 1) * P, half * HALF : (half + 1) * HALF],
                     in_=result[:].rearrange("p v d -> p (v d)"),
                 )
 
-        w2_q = (w2_codes, w2_scales)
         w3_bf, dst, src = group_views("w3_bf", w3_raw)
         nc.vector.tensor_scalar(out=dst, in0=src, scalar1=1.0 / D, scalar2=None, op0=ALU.mult)
         read_even(0)
         read_even(1)
-        add_odd(0)
-        add_odd(1)
+        add_odd(0, 0)
+        w3_q = quantise("w3", w3_bf[:], N)
+        add_odd(0, 1)
+        w2_bf, dst, src = group_views("w2_bf", w2_raw)
+        mid = N // 8
+        nc.scalar.activation(out=dst[:, mid:], in_=src[:, mid:], func=ACT.Copy)
+        nc.vector.tensor_copy(out=dst[:, 0:mid], in_=src[:, 0:mid])
+        add_odd(1, 0)
+        pool(0)
+        add_odd(1, 1)
         round_all(0)
         round_all(1)
-        pool(0)
-        w3_q = quantise("w3", w3_bf[:], N)
         z_q0 = quantise_z(0)
-        h_q0 = quantise_h(0)
         pool(1)
-        head(0, h_q0, z_q0, False, ())
+        w2_q = quantise("w2", w2_bf[:], N)
         z_q1 = quantise_z(1)
+        h_q0 = quantise_h(0)
+        head(0, [h_q0], z_q0, ())
         h_q1 = quantise_h(1)
-        head(1, h_q1, z_q1, False, (1,))
+        head(1, [h_q1], z_q1, (1,))

@@ -51,7 +51,15 @@ def tile_picked_ypnseg_mean_p_kernel(tc, x_words, x_scales, w1, w2, w3, offs, ou
         nc.vector.memset(scale_rows[64:P, :].bitcast(I32), 0)
         picked_planes = sb("picked_planes", [P, PASSES, S], U8)
         nc.vector.memset(picked_planes[:].rearrange("p o s -> p (o s)").bitcast(I32), 0)
-        w1_raw = [load_rows("w1_raw%d" % o, w1[o * K_PASS : (o + 1) * K_PASS, :], "w1_raw%d" % o) for o in range(PASSES)]
+
+        def load_words(o, tag):
+            table = keep.tile([P, T], U32, name="x_sb%d" % o, tag=tag, align_bytes=64)
+            nc.sync.dma_start(out=table[:].bitcast(I32), in_=x_words[o].rearrange("p n t -> p (n t)").bitcast(I32))
+            return table
+
+        w1_raw = [load_rows("w1_raw0", w1[0:K_PASS, :], "w1_raw0")]
+        x_sb = [load_words(0, "x_sb0")]
+        w1_raw.append(load_rows("w1_raw1", w1[K_PASS:K, :], "w1_raw1"))
 
         picked_rows = sb("picked_rows", [P, S], U8)
         nc.vector.tensor_copy(picked_rows[:], scale_rows[:].indirect(offsets[:]))
@@ -61,9 +69,7 @@ def tile_picked_ypnseg_mean_p_kernel(tc, x_words, x_scales, w1, w2, w3, offs, ou
                 in_=picked_rows[8 * q : 8 * q + 8, :].bitcast(I32),
             )
 
-        x_sb = keep.tile([P, PASSES, T], U32, name="x_sb", tag="scale_rows", align_bytes=64)
-        for o in range(PASSES):
-            nc.sync.dma_start(out=x_sb[:, o, :].bitcast(I32), in_=x_words[o].rearrange("p n t -> p (n t)").bitcast(I32))
+        x_sb.append(load_words(1, "scale_rows"))
 
         def quantise(name, values, width):
             codes = sb(name + "_codes", [P, width], U32)
@@ -85,13 +91,15 @@ def tile_picked_ypnseg_mean_p_kernel(tc, x_words, x_scales, w1, w2, w3, offs, ou
                 both.append(quantise("w1_%d_%d" % (o, u), grouped[:], 2 * P))
             w1_q.append(both)
 
-        w3_raw = load_rows("w3_raw", w3, "w1_raw0")
-        w2_raw = load_rows("w2_raw", w2, "w1_raw1")
+        head_raw = keep.tile([P, 2, PACK, N], F32, name="head_raw", tag="w1_raw0", align_bytes=64)
+        w3_raw, w2_raw = head_raw[:, 0], head_raw[:, 1]
+        for raw, rows in ((w3_raw, w3), (w2_raw, w2)):
+            nc.sync.dma_start(out=raw, in_=rows.rearrange("(p j) c -> p j c", j=PACK))
 
         def group_views(name, raw):
             grouped = sb(name, [P, N * PACK], BF16)
             dst = grouped[:].rearrange("p (c i j) -> p c j i", i=4, j=PACK)
-            src = raw[:].rearrange("p j (c i) -> p c j i", i=4)
+            src = raw.rearrange("p j (c i) -> p c j i", i=4)
             return grouped, dst, src
 
         h_banks = [psum.tile([P, PACK, CHUNK], F32, name="h_bank%d" % c) for c in range(S // CHUNK)]
@@ -99,7 +107,7 @@ def tile_picked_ypnseg_mean_p_kernel(tc, x_words, x_scales, w1, w2, w3, offs, ou
             for half in range(HALVES):
                 picked = sb("picked%d_%d" % (o, half), [P, HALF], U32)
                 cols = HALF // 16
-                nc.vector.tensor_copy(picked[:], x_sb[:, o, :].indirect(offsets[:, half * cols : (half + 1) * cols]))
+                nc.vector.tensor_copy(picked[:], x_sb[o][:].indirect(offsets[:, half * cols : (half + 1) * cols]))
                 for cc in range(HALF // CHUNK):
                     c = half * (HALF // CHUNK) + cc
                     for t in range(PACK):

@@ -35,8 +35,12 @@ def tile_picked_ypnseg_mean_p_kernel(tc, x_words, x_scales, w1, w2, w3, offs, ou
         def sb(name, shape, dtype):
             return keep.tile(shape, dtype, name=name, align_bytes=64)
 
-        offsets = keep.tile([P, S // 16], U16, name="offsets")
-        nc.sync.dma_start(offsets[:], offs)
+        def load_words(o, tag):
+            table = keep.tile([P, T], U32, name="x_sb%d" % o, tag=tag, align_bytes=64)
+            nc.sync.dma_start(out=table[:].bitcast(I32), in_=x_words[o].rearrange("p n t -> p (n t)").bitcast(I32))
+            return table
+
+        x_sb = [load_words(0, "x_sb0")]
 
         def load_rows(name, rows, tag):
             raw = keep.tile([P, PACK, rows.shape[1]], F32, name=name, tag=tag, align_bytes=64)
@@ -47,18 +51,14 @@ def tile_picked_ypnseg_mean_p_kernel(tc, x_words, x_scales, w1, w2, w3, offs, ou
         nc.sync.dma_start(
             out=scale_rows[0:32, :].bitcast(I32), in_=x_scales.rearrange("o r n -> r o n").bitcast(I32)
         )
+        offsets = keep.tile([P, S // 16], U16, name="offsets")
+        nc.sync.dma_start(offsets[:], offs)
         nc.vector.memset(scale_rows[32:64, :].bitcast(I32), 0)
         nc.vector.memset(scale_rows[64:P, :].bitcast(I32), 0)
         picked_planes = sb("picked_planes", [P, PASSES, S], U8)
         nc.vector.memset(picked_planes[:].rearrange("p o s -> p (o s)").bitcast(I32), 0)
 
-        def load_words(o, tag):
-            table = keep.tile([P, T], U32, name="x_sb%d" % o, tag=tag, align_bytes=64)
-            nc.sync.dma_start(out=table[:].bitcast(I32), in_=x_words[o].rearrange("p n t -> p (n t)").bitcast(I32))
-            return table
-
         w1_raw = [load_rows("w1_raw0", w1[0:K_PASS, :], "w1_raw0")]
-        x_sb = [load_words(0, "x_sb0")]
         w1_raw.append(load_rows("w1_raw1", w1[K_PASS:K, :], "w1_raw1"))
 
         picked_rows = sb("picked_rows", [P, S], U8)

@@ -22,44 +22,51 @@ PASSES = K // K_PASS
 HALVES = 2
 HALF = S // HALVES
 CHUNK = 128
+BANKS = S // CHUNK
 CLOUDS = HALF // D
+PER = CHUNK // D
 M_TILES = N // P
+W2_GROUPS = N // 4
+W2_ON_VECTOR = 20
 
 
 def tile_picked_ypnseg_mean_p_kernel(tc, x_words, x_scales, w1, w2, w3, offs, out):
     nc = tc.nc
     with ExitStack() as ctx:
         keep = ctx.enter_context(tc.tile_pool(name="keep", bufs=1))
+        stage = ctx.enter_context(tc.tile_pool(name="stage", bufs=1))
         psum = ctx.enter_context(tc.psum_pool(name="psum", bufs=1))
 
         def sb(name, shape, dtype):
             return keep.tile(shape, dtype, name=name, align_bytes=64)
+
+        def staged(name, shape, dtype, offset):
+            return stage.tile(shape, dtype, name=name, align_bytes=64, offset=offset)
+
+        def load_rows(raw, rows):
+            nc.sync.dma_start(out=raw[:], in_=rows.rearrange("(p j) c -> p j c", j=PACK))
+            return raw
+
+        offsets = keep.tile([P, S // 16], U16, name="offsets")
+        nc.sync.dma_start(offsets[:], offs)
+
+        scale_rows = sb("scale_rows", [P, T], U8)
+        nc.sync.dma_start(
+            out=scale_rows[0:32, :].bitcast(I32), in_=x_scales.rearrange("o r n -> r o n").bitcast(I32)
+        )
+        nc.vector.memset(scale_rows[32:64, :].bitcast(I32), 0)
+        nc.vector.memset(scale_rows[64:P, :].bitcast(I32), 0)
+        picked_planes = sb("picked_planes", [P, PASSES, S], U8)
+        nc.vector.memset(picked_planes[:].rearrange("p o s -> p (o s)").bitcast(I32), 0)
 
         def load_words(o, tag):
             table = keep.tile([P, T], U32, name="x_sb%d" % o, tag=tag, align_bytes=64)
             nc.sync.dma_start(out=table[:].bitcast(I32), in_=x_words[o].rearrange("p n t -> p (n t)").bitcast(I32))
             return table
 
+        w1_raw = [load_rows(keep.tile([P, PACK, H], F32, name="w1_raw0", tag="w1_raw0", align_bytes=64), w1[0:K_PASS, :])]
         x_sb = [load_words(0, "x_sb0")]
-
-        def load_rows(name, rows, tag):
-            raw = keep.tile([P, PACK, rows.shape[1]], F32, name=name, tag=tag, align_bytes=64)
-            nc.sync.dma_start(out=raw[:], in_=rows.rearrange("(p j) c -> p j c", j=PACK))
-            return raw
-
-        scale_rows = sb("scale_rows", [P, T], U8)
-        nc.sync.dma_start(
-            out=scale_rows[0:32, :].bitcast(I32), in_=x_scales.rearrange("o r n -> r o n").bitcast(I32)
-        )
-        offsets = keep.tile([P, S // 16], U16, name="offsets")
-        nc.sync.dma_start(offsets[:], offs)
-        nc.vector.memset(scale_rows[32:64, :].bitcast(I32), 0)
-        nc.vector.memset(scale_rows[64:P, :].bitcast(I32), 0)
-        picked_planes = sb("picked_planes", [P, PASSES, S], U8)
-        nc.vector.memset(picked_planes[:].rearrange("p o s -> p (o s)").bitcast(I32), 0)
-
-        w1_raw = [load_rows("w1_raw0", w1[0:K_PASS, :], "w1_raw0")]
-        w1_raw.append(load_rows("w1_raw1", w1[K_PASS:K, :], "w1_raw1"))
+        w1_raw.append(load_rows(sb("w1_raw1", [P, PACK, H], F32), w1[K_PASS:K, :]))
 
         picked_rows = sb("picked_rows", [P, S], U8)
         nc.vector.tensor_copy(picked_rows[:], scale_rows[:].indirect(offsets[:]))
@@ -71,9 +78,12 @@ def tile_picked_ypnseg_mean_p_kernel(tc, x_words, x_scales, w1, w2, w3, offs, ou
 
         x_sb.append(load_words(1, "scale_rows"))
 
-        def quantise(name, values, width):
+        def quantise(name, values, width, offset=None):
             codes = sb(name + "_codes", [P, width], U32)
-            scales = sb(name + "_scales", [P, width], U8)
+            if offset is None:
+                scales = sb(name + "_scales", [P, width], U8)
+            else:
+                scales = staged(name + "_scales", [P, width], U8, offset)
             nc.vector.quantize_mx(out=codes[:].bitcast(FP8X4), scales=scales[:], in_=values)
             return codes, scales
 
@@ -92,105 +102,91 @@ def tile_picked_ypnseg_mean_p_kernel(tc, x_words, x_scales, w1, w2, w3, offs, ou
             w1_q.append(both)
 
         head_raw = keep.tile([P, 2, PACK, N], F32, name="head_raw", tag="w1_raw0", align_bytes=64)
-        w3_raw, w2_raw = head_raw[:, 0], head_raw[:, 1]
-        for raw, rows in ((w3_raw, w3), (w2_raw, w2)):
-            nc.sync.dma_start(out=raw, in_=rows.rearrange("(p j) c -> p j c", j=PACK))
+        w3_raw, w2_raw = load_rows(head_raw[:, 0], w3), load_rows(head_raw[:, 1], w2)
 
-        def group_views(name, raw):
-            grouped = sb(name, [P, N * PACK], BF16)
+        def group_views(grouped, raw):
             dst = grouped[:].rearrange("p (c i j) -> p c j i", i=4, j=PACK)
-            src = raw.rearrange("p j (c i) -> p c j i", i=4)
+            src = raw[:].rearrange("p j (c i) -> p c j i", i=4)
             return grouped, dst, src
 
-        h_banks = [psum.tile([P, PACK, CHUNK], F32, name="h_bank%d" % c) for c in range(S // CHUNK)]
-        for o in range(PASSES):
-            for half in range(HALVES):
-                picked = sb("picked%d_%d" % (o, half), [P, HALF], U32)
-                cols = HALF // 16
-                nc.vector.tensor_copy(picked[:], x_sb[o][:].indirect(offsets[:, half * cols : (half + 1) * cols]))
-                for cc in range(HALF // CHUNK):
-                    c = half * (HALF // CHUNK) + cc
-                    for t in range(PACK):
-                        codes, scales = w1_q[o][t // 2]
-                        tc_cols = slice((t % 2) * P, (t % 2 + 1) * P)
-                        nc.tensor.matmul_mx(
-                            out=h_banks[c][:, t, :],
-                            lhsT=codes[:, tc_cols].bitcast(FP8X4),
-                            lhsT_scale=scales[:, tc_cols],
-                            rhs=picked[:, cc * CHUNK : (cc + 1) * CHUNK].bitcast(FP8X4),
-                            rhs_scale=picked_planes[:, o, c * CHUNK : (c + 1) * CHUNK],
-                            start=(o == 0 and t == 0),
-                            stop=(o == PASSES - 1 and t == PACK - 1),
-                        )
+        h_banks = [psum.tile([P, PACK, CHUNK], F32, name="h_bank%d" % c) for c in range(BANKS)]
 
-        per = CHUNK // D
-        banks_a_half = HALF // CHUNK
-        all_pairs = keep.tile([P, HALVES, HALF // 2, PACK], F32, name="pairs", align_bytes=64)
-        even, pairs, h_bf, z_bf = [], [], [], []
-        for half in range(HALVES):
-            even.append(sb("even%d" % half, [P, HALF // 2, PACK], F32))
-            pairs.append(all_pairs[:, half])
-            h_bf.append(sb("h_bf%d" % half, [P, D, CLOUDS, PACK], BF16))
-            z_bf.append(sb("z_bf%d" % half, [P, CLOUDS, PACK], BF16))
+        def gather(picked, o, first, count):
+            nc.vector.tensor_copy(picked[:], x_sb[o][:].indirect(offsets[:, first // 16 : (first + count) // 16]))
+            return picked
 
-        def banks_of(half):
-            return enumerate(h_banks[half * banks_a_half : (half + 1) * banks_a_half])
-
-        def read_even(half):
-            for cc, bank in banks_of(half):
-                ss = slice(cc * CHUNK // 2, (cc + 1) * CHUNK // 2)
-                by_parity = bank[:].rearrange("p t (s e) -> p e s t", e=2)
-                nc.scalar.activation(out=even[half][:, ss, :], in_=by_parity[:, 0], func=ACT.Relu)
-
-        def add_odd(half, cc):
-            for bank in h_banks[half * banks_a_half + cc : half * banks_a_half + cc + 1]:
-                ss = slice(cc * CHUNK // 2, (cc + 1) * CHUNK // 2)
-                by_parity = bank[:].rearrange("p t (s e) -> p e s t", e=2)
-                nc.vector.scalar_tensor_tensor(
-                    out=pairs[half][:, ss, :],
-                    in0=by_parity[:, 1],
-                    scalar=0.0,
-                    in1=even[half][:, ss, :],
-                    op0=ALU.max,
-                    op1=ALU.add,
+        def first_product(c, o, words, start, stop):
+            for t in range(PACK):
+                codes, scales = w1_q[o][t // 2]
+                cols = slice((t % 2) * P, (t % 2 + 1) * P)
+                nc.tensor.matmul_mx(
+                    out=h_banks[c][:, t, :],
+                    lhsT=codes[:, cols].bitcast(FP8X4),
+                    lhsT_scale=scales[:, cols],
+                    rhs=words.bitcast(FP8X4),
+                    rhs_scale=picked_planes[:, o, c * CHUNK : (c + 1) * CHUNK],
+                    start=(start and t == 0),
+                    stop=(stop and t == PACK - 1),
                 )
 
-        def round_odd(half):
-            h_rows = h_bf[half][:].rearrange("p (f e) v t -> p e f v t", e=2)
-            for cc, bank in banks_of(half):
-                odd = bank[:].rearrange("p t (v f e) -> p e f v t", f=2, e=2)[:, 1]
-                nc.scalar.activation(out=h_rows[:, 1, :, cc * per : (cc + 1) * per, :], in_=odd, func=ACT.Relu)
+        even = [
+            staged("even%d" % c, [P, CHUNK // 2, PACK], F32, 0) if c == 1 else sb("even%d" % c, [P, CHUNK // 2, PACK], F32)
+            for c in range(BANKS)
+        ]
+        pairs = [sb("pairs%d" % half, [P, HALF // 2, PACK], F32) for half in range(HALVES)]
+        h_bf = [sb("h_bf%d" % half, [P, D, CLOUDS, PACK], BF16) for half in range(HALVES)]
+        z_bf = [staged("z_bf0", [P, CLOUDS, PACK], BF16, 256), sb("z_bf1", [P, CLOUDS, PACK], BF16)]
 
-        def round_even(half):
-            h_rows = h_bf[half][:].rearrange("p (f e) v t -> p e f v t", e=2)
-            nc.vector.tensor_copy(out=h_rows[:, 0], in_=even[half][:].rearrange("p (v f) t -> p f v t", f=2))
+        def by_parity(c):
+            return h_banks[c][:].rearrange("p t (s e) -> p e s t", e=2)
 
-        def round_all(half):
-            for cc, bank in banks_of(half):
-                nc.scalar.activation(
-                    out=h_bf[half][:, :, cc * per : (cc + 1) * per, :],
-                    in_=bank[:].rearrange("p t (v d) -> p d v t", d=D),
-                    func=ACT.Relu,
-                )
+        def read_even(c):
+            nc.scalar.activation(out=even[c][:], in_=by_parity(c)[:, 0], func=ACT.Relu)
 
-        def round_rows(half, cc, rows):
-            bank = h_banks[half * banks_a_half + cc]
+        def add_odd(c):
+            half, cc = divmod(c, 2)
+            nc.vector.scalar_tensor_tensor(
+                out=pairs[half][:, cc * CHUNK // 2 : (cc + 1) * CHUNK // 2, :],
+                in0=by_parity(c)[:, 1],
+                scalar=0.0,
+                in1=even[c][:],
+                op0=ALU.max,
+                op1=ALU.add,
+            )
+
+        def round_h(c, rows):
+            half, cc = divmod(c, 2)
             nc.scalar.activation(
-                out=h_bf[half][:, rows, cc * per : (cc + 1) * per, :],
-                in_=bank[:].rearrange("p t (v d) -> p d v t", d=D)[:, rows],
+                out=h_bf[half][:, rows, cc * PER : (cc + 1) * PER, :],
+                in_=h_banks[c][:].rearrange("p t (v d) -> p d v t", d=D)[:, rows],
                 func=ACT.Relu,
             )
 
-        def quantise_rows(half, e):
-            rows = h_bf[half][:, 2 * e : 2 * e + 2].rearrange("p d v t -> p (d v t)")
-            return quantise("h%d_%d" % (half, e), rows, P)
+        def parity_rows(c):
+            half, cc = divmod(c, 2)
+            return h_bf[half][:].rearrange("p (f e) v t -> p e f v t", e=2)[:, :, :, cc * PER : (cc + 1) * PER, :]
+
+        def round_even(c):
+            nc.gpsimd.tensor_scalar(
+                out=parity_rows(c)[:, 0],
+                in0=even[c][:].rearrange("p (v f) t -> p f v t", f=2),
+                scalar1=1.0,
+                scalar2=0.0,
+                op0=ALU.mult,
+                op1=ALU.add,
+            )
+
+        def round_odd(c):
+            odd = h_banks[c][:].rearrange("p t (v f e) -> p e f v t", f=2, e=2)[:, 1]
+            nc.scalar.activation(out=parity_rows(c)[:, 1], in_=odd, func=ACT.Relu)
 
         def pool(half):
-            by_cloud = pairs[half].rearrange("p (v f) t -> p f v t", f=2)
+            by_cloud = pairs[half][:].rearrange("p (v f) t -> p f v t", f=2)
             nc.vector.tensor_tensor(out=z_bf[half][:], in0=by_cloud[:, 0], in1=by_cloud[:, 1], op=ALU.add)
 
-        def quantise_h(half):
-            return quantise("h%d" % half, h_bf[half][:].rearrange("p d v t -> p (d v t)"), HALF)
+        def quantise_h(half, rows):
+            values = h_bf[half][:, rows].rearrange("p d v t -> p (d v t)")
+            return quantise("h%d_%d" % (half, rows.start), values, (rows.stop - rows.start) * CLOUDS)
 
         def quantise_z(half):
             z_codes = sb("z_codes%d" % half, [P, 2 * CLOUDS], U32)
@@ -204,6 +200,8 @@ def tile_picked_ypnseg_mean_p_kernel(tc, x_words, x_scales, w1, w2, w3, offs, ou
                 )
             return z_codes, z_scales
 
+        accs = [[psum.tile([P, HALF], F32, name="acc%d_%d" % (half, m)) for m in range(M_TILES)] for half in range(HALVES)]
+
         def product(acc, weights, m, values, start, stop):
             mc = slice(m * P, (m + 1) * P)
             nc.tensor.matmul_mx(
@@ -216,50 +214,64 @@ def tile_picked_ypnseg_mean_p_kernel(tc, x_words, x_scales, w1, w2, w3, offs, ou
                 stop=stop,
             )
 
-        def head(half, h_q, z_q, on_vector):
-            accs = [psum.tile([P, HALF], F32, name="acc%d_%d" % (half, m), tag="acc%d_%d" % (half, m)) for m in range(M_TILES)]
-            for m, acc in enumerate(accs):
-                for e in range(2):
-                    product(acc[:, e * P : (e + 1) * P], w3_q, m, z_q, e == 0, False)
-            width = HALF // len(h_q)
-            for e, piece in enumerate(h_q[:-1]):
-                for m, acc in enumerate(accs):
-                    product(acc[:, e * width : (e + 1) * width], w2_q, m, piece, False, False)
-            for m, acc in enumerate(accs):
-                product(acc[:, HALF - width :], w2_q, m, h_q[-1], False, True)
-                result = sb("result%d_%d" % (half, m), [P, CLOUDS, D], F32)
-                ordered = acc[:].rearrange("p (d v) -> p v d", d=D)
-                if m in on_vector:
-                    nc.vector.tensor_scalar(out=result[:], in0=ordered, scalar1=0.0, scalar2=None, op0=ALU.max)
-                else:
-                    nc.scalar.activation(out=result[:], in_=ordered, func=ACT.Relu)
-                queue = nc.sync
-                queue.dma_start(
-                    out=out[m * P : (m + 1) * P, half * HALF : (half + 1) * HALF],
-                    in_=result[:].rearrange("p v d -> p (v d)"),
-                )
+        def pooled_product(half, z_q, columns, start, stop):
+            for m in range(M_TILES):
+                for e in columns:
+                    product(accs[half][m][:, e * P : (e + 1) * P], w3_q, m, z_q, start and e == columns[0], stop and e == columns[-1])
 
-        w3_bf, dst, src = group_views("w3_bf", w3_raw)
+        def own_product(half, rows, h_q, start, stop):
+            for m in range(M_TILES):
+                product(accs[half][m][:, rows.start * CLOUDS : rows.stop * CLOUDS], w2_q, m, h_q, start, stop)
+
+        def leave(half, m, on_vector):
+            result = sb("result%d_%d" % (half, m), [P, CLOUDS, D], F32)
+            ordered = accs[half][m][:].rearrange("p (d v) -> p v d", d=D)
+            if on_vector:
+                nc.vector.tensor_scalar(out=result[:], in0=ordered, scalar1=0.0, scalar2=None, op0=ALU.max)
+            else:
+                nc.scalar.activation(out=result[:], in_=ordered, func=ACT.Relu)
+            nc.sync.dma_start(
+                out=out[m * P : (m + 1) * P, half * HALF : (half + 1) * HALF],
+                in_=result[:].rearrange("p v d -> p (v d)"),
+            )
+
+        def clock(name, ap):
+            t = sb(name, [P, 1], ap.dtype)
+            nc.gpsimd.tensor_copy(out=t[:], in_=ap)
+
+        all_rows, low_rows, high_rows = slice(0, D), slice(0, D // 2), slice(D // 2, D)
+
+        for o in range(PASSES):
+            for half in range(HALVES):
+                picked = gather(sb("picked%d_%d" % (o, half), [P, HALF], U32), o, half * HALF, HALF)
+                for cc in range(2):
+                    first_product(2 * half + cc, o, picked[:, cc * CHUNK : (cc + 1) * CHUNK], o == 0, o == PASSES - 1)
+
+        w3_bf, dst, src = group_views(sb("w3_bf", [P, N * PACK], BF16), w3_raw)
         nc.vector.tensor_scalar(out=dst, in0=src, scalar1=1.0 / D, scalar2=None, op0=ALU.mult)
-        read_even(0)
-        read_even(1)
-        add_odd(0, 0)
-        w3_q = quantise("w3", w3_bf[:], N)
-        add_odd(0, 1)
-        w2_bf, dst, src = group_views("w2_bf", w2_raw)
-        mid = N // 8
-        nc.scalar.activation(out=dst[:, mid:], in_=src[:, mid:], func=ACT.Copy)
-        nc.vector.tensor_copy(out=dst[:, 0:mid], in_=src[:, 0:mid])
-        add_odd(1, 0)
+        for c in range(BANKS):
+            read_even(c)
+        for c in range(BANKS):
+            add_odd(c)
+        for c in range(2):
+            round_even(c)
+            round_odd(c)
+        w3_q = quantise("w3", w3_bf[:], N, 0)
         pool(0)
-        add_odd(1, 1)
-        round_all(0)
-        round_all(1)
-        z_q0 = quantise_z(0)
+        w2_bf, dst, src = group_views(staged("w2_bf", [P, N * PACK], BF16, 768), w2_raw)
+        nc.scalar.activation(out=dst[:, W2_ON_VECTOR:], in_=src[:, W2_ON_VECTOR:], func=ACT.Copy)
+        nc.vector.tensor_copy(out=dst[:, 0:W2_ON_VECTOR], in_=src[:, 0:W2_ON_VECTOR])
+        round_h(2, all_rows)
+        round_h(3, all_rows)
+        pooled_product(0, quantise_z(0), (0, 1), True, False)
         pool(1)
-        w2_q = quantise("w2", w2_bf[:], N)
+        h_q0 = quantise_h(0, all_rows)
         z_q1 = quantise_z(1)
-        h_q0 = quantise_h(0)
-        head(0, [h_q0], z_q0, ())
-        h_q1 = quantise_h(1)
-        head(1, [h_q1], z_q1, (1,))
+        w2_q = quantise("w2", w2_bf[:], N)
+        pooled_product(1, z_q1, (0, 1), True, False)
+        own_product(0, all_rows, h_q0, False, True)
+        own_product(1, all_rows, quantise_h(1, all_rows), False, True)
+        leave(0, 0, False)
+        leave(0, 1, False)
+        leave(1, 0, False)
+        leave(1, 1, True)

@@ -27,7 +27,7 @@ CLOUDS = HALF // D
 PER = CHUNK // D
 M_TILES = N // P
 W2_GROUPS = N // 4
-W2_ON_VECTOR = 20
+W2_ON_VECTOR = 24
 
 
 def tile_picked_ypnseg_mean_p_kernel(tc, x_words, x_scales, w1, w2, w3, offs, out):
@@ -262,15 +262,16 @@ def tile_picked_ypnseg_mean_p_kernel(tc, x_words, x_scales, w1, w2, w3, offs, ou
         nc.scalar.activation(out=dst[:, W2_ON_VECTOR:], in_=src[:, W2_ON_VECTOR:], func=ACT.Copy)
         nc.vector.tensor_copy(out=dst[:, 0:W2_ON_VECTOR], in_=src[:, 0:W2_ON_VECTOR])
         round_h(2, all_rows)
-        round_h(3, all_rows)
+        round_h(3, low_rows)
+        round_h(3, high_rows)
         pooled_product(0, quantise_z(0), (0, 1), True, False)
         pool(1)
         h_q0 = quantise_h(0, all_rows)
-        z_q1 = quantise_z(1)
         w2_q = quantise("w2", w2_bf[:], N)
-        pooled_product(1, z_q1, (0, 1), True, False)
         own_product(0, all_rows, h_q0, False, True)
-        own_product(1, all_rows, quantise_h(1, all_rows), False, True)
+        pooled_product(1, quantise_z(1), (0, 1), True, False)
+        own_product(1, low_rows, quantise_h(1, low_rows), False, False)
+        own_product(1, high_rows, quantise_h(1, high_rows), False, True)
         leave(0, 0, False)
         leave(0, 1, False)
         leave(1, 0, False)

@@ -257,6 +257,8 @@ def tile_picked_ypnseg_mean_p_kernel(tc, x_words, x_scales, w1, w2, w3, offs, ou
             round_even(c)
             round_odd(c)
         w3_q = quantise("w3", w3_bf[:], N, 0)
+        for m in range(M_TILES):
+            product(accs[1][m][:], w3_q, m, w3_q, True, True)
         pool(0)
         w2_bf, dst, src = group_views(staged("w2_bf", [P, N * PACK], BF16, 768), w2_raw)
         nc.scalar.activation(out=dst[:, W2_ON_VECTOR:], in_=src[:, W2_ON_VECTOR:], func=ACT.Copy)

@@ -109,7 +109,7 @@ def tile_picked_ypnseg_mean_p_kernel(tc, x_words, x_scales, w1, w2, w3, offs, ou
             src = raw[:].rearrange("p j (c i) -> p c j i", i=4)
             return grouped, dst, src
 
-        h_banks = [psum.tile([P, PACK, CHUNK], F32, name="h_bank%d" % c) for c in range(BANKS)]
+        h_banks = [psum.tile([P, PACK, CHUNK], F32, name="h_bank%d" % c, tag="h_bank%d" % c) for c in range(BANKS)]
 
         def gather(picked, o, first, count):
             nc.vector.tensor_copy(picked[:], x_sb[o][:].indirect(offsets[:, first // 16 : (first + count) // 16]))
@@ -235,10 +235,6 @@ def tile_picked_ypnseg_mean_p_kernel(tc, x_words, x_scales, w1, w2, w3, offs, ou
                 in_=result[:].rearrange("p v d -> p (v d)"),
             )
 
-        def clock(name, ap):
-            t = sb(name, [P, 1], ap.dtype)
-            nc.gpsimd.tensor_copy(out=t[:], in_=ap)
-
         all_rows, low_rows, high_rows = slice(0, D), slice(0, D // 2), slice(D // 2, D)
 
         for o in range(PASSES):
@@ -256,17 +252,18 @@ def tile_picked_ypnseg_mean_p_kernel(tc, x_words, x_scales, w1, w2, w3, offs, ou
         for c in range(2):
             round_even(c)
             round_odd(c)
-        w3_q = quantise("w3", w3_bf[:], N, 0)
+        idle_bank = psum.tile([P, M_TILES, HALF], F32, name="idle_bank", tag="h_bank0")
         for m in range(M_TILES):
-            product(accs[1][m][:], w3_q, m, w3_q, True, True)
+            product(idle_bank[:, m, :], w1_q[0][0], m, w1_q[0][0], True, True)
         pool(0)
+        w3_q = quantise("w3", w3_bf[:], N, 0)
+        pooled_product(0, quantise_z(0), (0, 1), True, False)
         w2_bf, dst, src = group_views(staged("w2_bf", [P, N * PACK], BF16, 768), w2_raw)
         nc.scalar.activation(out=dst[:, W2_ON_VECTOR:], in_=src[:, W2_ON_VECTOR:], func=ACT.Copy)
         nc.vector.tensor_copy(out=dst[:, 0:W2_ON_VECTOR], in_=src[:, 0:W2_ON_VECTOR])
         round_h(2, all_rows)
         round_h(3, low_rows)
         round_h(3, high_rows)
-        pooled_product(0, quantise_z(0), (0, 1), True, False)
         pool(1)
         h_q0 = quantise_h(0, all_rows)
         w2_q = quantise("w2", w2_bf[:], N)

@@ -135,7 +135,7 @@ def tile_picked_ypnseg_mean_p_kernel(tc, x_words, x_scales, w1, w2, w3, offs, ou
         ]
         pairs = [sb("pairs%d" % half, [P, HALF // 2, PACK], F32) for half in range(HALVES)]
         h_bf = [sb("h_bf%d" % half, [P, D, CLOUDS, PACK], BF16) for half in range(HALVES)]
-        z_bf = [staged("z_bf0", [P, CLOUDS, PACK], BF16, 256), sb("z_bf1", [P, CLOUDS, PACK], BF16)]
+        z_bf = [sb("z_bf0", [P, CLOUDS, PACK], BF16), sb("z_bf1", [P, CLOUDS, PACK], BF16)]
 
         def by_parity(c):
             return h_banks[c][:].rearrange("p t (s e) -> p e s t", e=2)
@@ -247,7 +247,7 @@ def tile_picked_ypnseg_mean_p_kernel(tc, x_words, x_scales, w1, w2, w3, offs, ou
         nc.vector.tensor_scalar(out=dst, in0=src, scalar1=1.0 / D, scalar2=None, op0=ALU.mult)
         for c in range(BANKS):
             read_even(c)
-        for c in range(BANKS):
+        for c in range(BANKS - 1):
             add_odd(c)
         for c in range(2):
             round_even(c)
@@ -258,6 +258,7 @@ def tile_picked_ypnseg_mean_p_kernel(tc, x_words, x_scales, w1, w2, w3, offs, ou
         pool(0)
         w3_q = quantise("w3", w3_bf[:], N, 0)
         pooled_product(0, quantise_z(0), (0, 1), True, False)
+        add_odd(BANKS - 1)
         w2_bf, dst, src = group_views(staged("w2_bf", [P, N * PACK], BF16, 768), w2_raw)
         nc.scalar.activation(out=dst[:, W2_ON_VECTOR:], in_=src[:, W2_ON_VECTOR:], func=ACT.Copy)
         nc.vector.tensor_copy(out=dst[:, 0:W2_ON_VECTOR], in_=src[:, 0:W2_ON_VECTOR])
@@ -272,6 +273,6 @@ def tile_picked_ypnseg_mean_p_kernel(tc, x_words, x_scales, w1, w2, w3, offs, ou
         own_product(1, low_rows, quantise_h(1, low_rows), False, False)
         own_product(1, high_rows, quantise_h(1, high_rows), False, True)
         leave(0, 0, False)
-        leave(0, 1, False)
+        leave(0, 1, True)
         leave(1, 0, False)
         leave(1, 1, True)

@@ -27,7 +27,7 @@ CLOUDS = HALF // D
 PER = CHUNK // D
 M_TILES = N // P
 W2_GROUPS = N // 4
-W2_ON_VECTOR = 24
+W2_ON_VECTOR = 12
 
 
 def tile_picked_ypnseg_mean_p_kernel(tc, x_words, x_scales, w1, w2, w3, offs, out):
@@ -70,7 +70,7 @@ def tile_picked_ypnseg_mean_p_kernel(tc, x_words, x_scales, w1, w2, w3, offs, ou
 
         picked_rows = sb("picked_rows", [P, S], U8)
         nc.vector.tensor_copy(picked_rows[:], scale_rows[:].indirect(offsets[:]))
-        for q in range(4):
+        for q in (0, 2, 1, 3):
             nc.sync.dma_start(
                 out=picked_planes[32 * q : 32 * q + 4].rearrange("p o s -> p (o s)").bitcast(I32),
                 in_=picked_rows[8 * q : 8 * q + 8, :].bitcast(I32),

@@ -265,13 +265,17 @@ def tile_picked_ypnseg_mean_p_kernel(tc, x_words, x_scales, w1, w2, w3, offs, ou
         round_h(2, all_rows)
         round_h(3, low_rows)
         round_h(3, high_rows)
-        pool(1)
         h_q0 = quantise_h(0, all_rows)
         w2_q = quantise("w2", w2_bf[:], N)
         own_product(0, all_rows, h_q0, False, True)
-        pooled_product(1, quantise_z(1), (0, 1), True, False)
-        own_product(1, low_rows, quantise_h(1, low_rows), False, False)
-        own_product(1, high_rows, quantise_h(1, high_rows), False, True)
+        pool(1)
+        own_product(1, low_rows, quantise_h(1, low_rows), True, False)
+        z_q1 = quantise_z(1)
+        h_q1 = quantise_h(1, high_rows)
+        for m in range(M_TILES):
+            for e in range(2):
+                product(accs[1][m][:, e * P : (e + 1) * P], w3_q, m, z_q1, False, False)
+            product(accs[1][m][:, P : 2 * P], w2_q, m, h_q1, False, True)
         leave(0, 0, False)
         leave(0, 1, True)
         leave(1, 0, False)

@@ -26,6 +26,7 @@ BANKS = S // CHUNK
 CLOUDS = HALF // D
 PER = CHUNK // D
 M_TILES = N // P
+RAW_BYTES = 4 * T
 W2_GROUPS = N // 4
 W2_ON_VECTOR = 12
 
@@ -35,6 +36,8 @@ def tile_picked_ypnseg_mean_p_kernel(tc, x_words, x_scales, w1, w2, w3, offs, ou
     with ExitStack() as ctx:
         keep = ctx.enter_context(tc.tile_pool(name="keep", bufs=1))
         stage = ctx.enter_context(tc.tile_pool(name="stage", bufs=1))
+        early = ctx.enter_context(tc.tile_pool(name="early", bufs=1))
+        late = ctx.enter_context(tc.tile_pool(name="late", bufs=1))
         psum = ctx.enter_context(tc.psum_pool(name="psum", bufs=1))
 
         def sb(name, shape, dtype):
@@ -50,7 +53,7 @@ def tile_picked_ypnseg_mean_p_kernel(tc, x_words, x_scales, w1, w2, w3, offs, ou
         offsets = keep.tile([P, S // 16], U16, name="offsets")
         nc.sync.dma_start(offsets[:], offs)
 
-        scale_rows = sb("scale_rows", [P, T], U8)
+        scale_rows = late.tile([P, T], U8, name="scale_rows", align_bytes=64, offset=RAW_BYTES - T // 2)
         nc.sync.dma_start(
             out=scale_rows[0:32, :].bitcast(I32), in_=x_scales.rearrange("o r n -> r o n").bitcast(I32)
         )
@@ -59,14 +62,12 @@ def tile_picked_ypnseg_mean_p_kernel(tc, x_words, x_scales, w1, w2, w3, offs, ou
         picked_planes = sb("picked_planes", [P, PASSES, S], U8)
         nc.vector.memset(picked_planes[:].rearrange("p o s -> p (o s)").bitcast(I32), 0)
 
-        def load_words(o, tag):
-            table = keep.tile([P, T], U32, name="x_sb%d" % o, tag=tag, align_bytes=64)
+        def load_words(o, table):
             nc.sync.dma_start(out=table[:].bitcast(I32), in_=x_words[o].rearrange("p n t -> p (n t)").bitcast(I32))
             return table
 
-        w1_raw = [load_rows(keep.tile([P, PACK, H], F32, name="w1_raw0", tag="w1_raw0", align_bytes=64), w1[0:K_PASS, :])]
-        x_sb = [load_words(0, "x_sb0")]
-        w1_raw.append(load_rows(sb("w1_raw1", [P, PACK, H], F32), w1[K_PASS:K, :]))
+        x_sb = [load_words(0, sb("x_sb0", [P, T], U32))]
+        w1_raw = [load_rows(early.tile([P, PACK, H], F32, name="w1_raw0", align_bytes=64, offset=2048), w1[0:K_PASS, :])]
 
         picked_rows = sb("picked_rows", [P, S], U8)
         nc.vector.tensor_copy(picked_rows[:], scale_rows[:].indirect(offsets[:]))
@@ -75,8 +76,8 @@ def tile_picked_ypnseg_mean_p_kernel(tc, x_words, x_scales, w1, w2, w3, offs, ou
                 out=picked_planes[32 * q : 32 * q + 4].rearrange("p o s -> p (o s)").bitcast(I32),
                 in_=picked_rows[8 * q : 8 * q + 8, :].bitcast(I32),
             )
-
-        x_sb.append(load_words(1, "scale_rows"))
+        w1_raw.append(load_rows(late.tile([P, PACK, H], F32, name="w1_raw1", align_bytes=64, offset=0), w1[K_PASS:K, :]))
+        x_sb.append(load_words(1, late.tile([P, T], U32, name="x_sb1", align_bytes=64, offset=RAW_BYTES)))
 
         def quantise(name, values, width, offset=None):
             codes = sb(name + "_codes", [P, width], U32)
@@ -94,15 +95,15 @@ def tile_picked_ypnseg_mean_p_kernel(tc, x_words, x_scales, w1, w2, w3, offs, ou
             for u in range(2):
                 grouped = sb("w1_bf%d_%d" % (o, u), [P, 2 * P * PACK], BF16)
                 dst = grouped[:].rearrange("p (t m j) -> p m j t", t=2, j=PACK)
-                if u == 0:
-                    nc.vector.tensor_copy(out=dst, in_=src[:, :, :, 0:2])
+                if u != o:
+                    nc.vector.tensor_copy(out=dst, in_=src[:, :, :, 2 * u : 2 * u + 2])
                 else:
-                    nc.scalar.activation(out=dst, in_=src[:, :, :, 2:4], func=ACT.Copy)
+                    nc.scalar.activation(out=dst, in_=src[:, :, :, 2 * u : 2 * u + 2], func=ACT.Copy)
                 both.append(quantise("w1_%d_%d" % (o, u), grouped[:], 2 * P))
             w1_q.append(both)
 
-        head_raw = keep.tile([P, 2, PACK, N], F32, name="head_raw", tag="w1_raw0", align_bytes=64)
-        w3_raw, w2_raw = load_rows(head_raw[:, 0], w3), load_rows(head_raw[:, 1], w2)
+        w3_raw = load_rows(early.tile([P, PACK, N], F32, name="w3_raw", align_bytes=64, offset=2048), w3)
+        w2_raw = load_rows(early.tile([P, PACK, N], F32, name="w2_raw", align_bytes=64, offset=6208), w2)
 
         def group_views(grouped, raw):
             dst = grouped[:].rearrange("p (c i j) -> p c j i", i=4, j=PACK)
@@ -133,8 +134,14 @@ def tile_picked_ypnseg_mean_p_kernel(tc, x_words, x_scales, w1, w2, w3, offs, ou
             staged("even%d" % c, [P, CHUNK // 2, PACK], F32, 0) if c == 1 else sb("even%d" % c, [P, CHUNK // 2, PACK], F32)
             for c in range(BANKS)
         ]
-        pairs = [sb("pairs%d" % half, [P, HALF // 2, PACK], F32) for half in range(HALVES)]
-        h_bf = [sb("h_bf%d" % half, [P, D, CLOUDS, PACK], BF16) for half in range(HALVES)]
+        pairs = [
+            early.tile([P, HALF // 2, PACK], F32, name="pairs0", align_bytes=64, offset=64),
+            early.tile([P, HALF // 2, PACK], F32, name="pairs1", align_bytes=64, offset=4160),
+        ]
+        h_bf = [
+            sb("h_bf0", [P, D, CLOUDS, PACK], BF16),
+            sb("h_bf1", [P, D, CLOUDS, PACK], BF16),
+        ]
         z_bf = [sb("z_bf0", [P, CLOUDS, PACK], BF16), sb("z_bf1", [P, CLOUDS, PACK], BF16)]
 
         def by_parity(c):

@@ -50,13 +50,13 @@ def tile_picked_ypnseg_mean_p_kernel(tc, x_words, x_scales, w1, w2, w3, offs, ou
             nc.sync.dma_start(out=raw[:], in_=rows.rearrange("(p j) c -> p j c", j=PACK))
             return raw
 
-        offsets = keep.tile([P, S // 16], U16, name="offsets")
-        nc.sync.dma_start(offsets[:], offs)
-
         scale_rows = late.tile([P, T], U8, name="scale_rows", align_bytes=64, offset=RAW_BYTES - T // 2)
         nc.sync.dma_start(
             out=scale_rows[0:32, :].bitcast(I32), in_=x_scales.rearrange("o r n -> r o n").bitcast(I32)
         )
+        offsets = keep.tile([P, S // 16], U16, name="offsets")
+        nc.sync.dma_start(offsets[:], offs)
+
         nc.vector.memset(scale_rows[32:64, :].bitcast(I32), 0)
         nc.vector.memset(scale_rows[64:P, :].bitcast(I32), 0)
         picked_planes = sb("picked_planes", [P, PASSES, S], U8)

from contextlib import ExitStack

import concourse.mybir as mybir

K, T, S, H, N, D = 1024, 2048, 512, 512, 256, 4
FLOPS = 2 * K * H * S + 2 * H * N * S + 2 * H * N * (S // D)

F32 = mybir.dt.float32
BF16 = mybir.dt.bfloat16
I32 = mybir.dt.int32
U32 = mybir.dt.uint32
U16 = mybir.dt.uint16
U8 = mybir.dt.uint8
FP8X4 = mybir.dt.float8_e4m3fn_x4
ACT = mybir.ActivationFunctionType
ALU = mybir.AluOpType

P = 128
PACK = 4
K_PASS = P * PACK
PASSES = K // K_PASS
HALVES = 2
HALF = S // HALVES
CHUNK = 128
BANKS = S // CHUNK
CLOUDS = HALF // D
PER = CHUNK // D
M_TILES = N // P
RAW_BYTES = 4 * T
W2_GROUPS = N // 4
W2_ON_VECTOR = 12


def tile_picked_ypnseg_mean_p_kernel(tc, x_words, x_scales, w1, w2, w3, offs, out):
    nc = tc.nc
    with ExitStack() as ctx:
        keep = ctx.enter_context(tc.tile_pool(name="keep", bufs=1))
        stage = ctx.enter_context(tc.tile_pool(name="stage", bufs=1))
        early = ctx.enter_context(tc.tile_pool(name="early", bufs=1))
        late = ctx.enter_context(tc.tile_pool(name="late", bufs=1))
        psum = ctx.enter_context(tc.psum_pool(name="psum", bufs=1))

        def sb(name, shape, dtype):
            return keep.tile(shape, dtype, name=name, align_bytes=64)

        def staged(name, shape, dtype, offset):
            return stage.tile(shape, dtype, name=name, align_bytes=64, offset=offset)

        def load_rows(raw, rows):
            nc.sync.dma_start(out=raw[:], in_=rows.rearrange("(p j) c -> p j c", j=PACK))
            return raw

        scale_rows = late.tile([P, T], U8, name="scale_rows", align_bytes=64, offset=RAW_BYTES - T // 2)
        nc.sync.dma_start(
            out=scale_rows[0:32, :].bitcast(I32), in_=x_scales.rearrange("o r n -> r o n").bitcast(I32)
        )
        offsets = keep.tile([P, S // 16], U16, name="offsets")
        nc.sync.dma_start(offsets[:], offs)

        nc.vector.memset(scale_rows[32:64, :].bitcast(I32), 0)
        nc.vector.memset(scale_rows[64:P, :].bitcast(I32), 0)
        picked_planes = sb("picked_planes", [P, PASSES, S], U8)
        nc.vector.memset(picked_planes[:].rearrange("p o s -> p (o s)").bitcast(I32), 0)

        def load_words(o, table):
            nc.sync.dma_start(out=table[:].bitcast(I32), in_=x_words[o].rearrange("p n t -> p (n t)").bitcast(I32))
            return table

        x_sb = [load_words(0, sb("x_sb0", [P, T], U32))]
        w1_raw = [load_rows(early.tile([P, PACK, H], F32, name="w1_raw0", align_bytes=64, offset=2048), w1[0:K_PASS, :])]

        picked_rows = sb("picked_rows", [P, S], U8)
        nc.vector.tensor_copy(picked_rows[:], scale_rows[:].indirect(offsets[:]))
        for q in (0, 2, 1, 3):
            nc.sync.dma_start(
                out=picked_planes[32 * q : 32 * q + 4].rearrange("p o s -> p (o s)").bitcast(I32),
                in_=picked_rows[8 * q : 8 * q + 8, :].bitcast(I32),
            )
        w1_raw.append(load_rows(late.tile([P, PACK, H], F32, name="w1_raw1", align_bytes=64, offset=0), w1[K_PASS:K, :]))
        x_sb.append(load_words(1, late.tile([P, T], U32, name="x_sb1", align_bytes=64, offset=RAW_BYTES)))

        def quantise(name, values, width, offset=None):
            codes = sb(name + "_codes", [P, width], U32)
            if offset is None:
                scales = sb(name + "_scales", [P, width], U8)
            else:
                scales = staged(name + "_scales", [P, width], U8, offset)
            nc.vector.quantize_mx(out=codes[:].bitcast(FP8X4), scales=scales[:], in_=values)
            return codes, scales

        w1_q = []
        for o in range(PASSES):
            src = w1_raw[o][:].rearrange("p j (m t) -> p m j t", t=PACK)
            both = []
            for u in range(2):
                grouped = sb("w1_bf%d_%d" % (o, u), [P, 2 * P * PACK], BF16)
                dst = grouped[:].rearrange("p (t m j) -> p m j t", t=2, j=PACK)
                if u != o:
                    nc.vector.tensor_copy(out=dst, in_=src[:, :, :, 2 * u : 2 * u + 2])
                else:
                    nc.scalar.activation(out=dst, in_=src[:, :, :, 2 * u : 2 * u + 2], func=ACT.Copy)
                both.append(quantise("w1_%d_%d" % (o, u), grouped[:], 2 * P))
            w1_q.append(both)

        w3_raw = load_rows(early.tile([P, PACK, N], F32, name="w3_raw", align_bytes=64, offset=2048), w3)
        w2_raw = load_rows(early.tile([P, PACK, N], F32, name="w2_raw", align_bytes=64, offset=6208), w2)

        def group_views(grouped, raw):
            dst = grouped[:].rearrange("p (c i j) -> p c j i", i=4, j=PACK)
            src = raw[:].rearrange("p j (c i) -> p c j i", i=4)
            return grouped, dst, src

        h_banks = [psum.tile([P, PACK, CHUNK], F32, name="h_bank%d" % c, tag="h_bank%d" % c) for c in range(BANKS)]

        def gather(picked, o, first, count):
            nc.vector.tensor_copy(picked[:], x_sb[o][:].indirect(offsets[:, first // 16 : (first + count) // 16]))
            return picked

        def first_product(c, o, words, start, stop):
            for t in range(PACK):
                codes, scales = w1_q[o][t // 2]
                cols = slice((t % 2) * P, (t % 2 + 1) * P)
                nc.tensor.matmul_mx(
                    out=h_banks[c][:, t, :],
                    lhsT=codes[:, cols].bitcast(FP8X4),
                    lhsT_scale=scales[:, cols],
                    rhs=words.bitcast(FP8X4),
                    rhs_scale=picked_planes[:, o, c * CHUNK : (c + 1) * CHUNK],
                    start=(start and t == 0),
                    stop=(stop and t == PACK - 1),
                )

        even = [
            staged("even%d" % c, [P, CHUNK // 2, PACK], F32, 0) if c == 1 else sb("even%d" % c, [P, CHUNK // 2, PACK], F32)
            for c in range(BANKS)
        ]
        pairs = [
            early.tile([P, HALF // 2, PACK], F32, name="pairs0", align_bytes=64, offset=64),
            early.tile([P, HALF // 2, PACK], F32, name="pairs1", align_bytes=64, offset=4160),
        ]
        h_bf = [
            sb("h_bf0", [P, D, CLOUDS, PACK], BF16),
            sb("h_bf1", [P, D, CLOUDS, PACK], BF16),
        ]
        z_bf = [sb("z_bf0", [P, CLOUDS, PACK], BF16), sb("z_bf1", [P, CLOUDS, PACK], BF16)]

        def by_parity(c):
            return h_banks[c][:].rearrange("p t (s e) -> p e s t", e=2)

        def read_even(c):
            nc.scalar.activation(out=even[c][:], in_=by_parity(c)[:, 0], func=ACT.Relu)

        def add_odd(c):
            half, cc = divmod(c, 2)
            nc.vector.scalar_tensor_tensor(
                out=pairs[half][:, cc * CHUNK // 2 : (cc + 1) * CHUNK // 2, :],
                in0=by_parity(c)[:, 1],
                scalar=0.0,
                in1=even[c][:],
                op0=ALU.max,
                op1=ALU.add,
            )

        def round_h(c, rows):
            half, cc = divmod(c, 2)
            nc.scalar.activation(
                out=h_bf[half][:, rows, cc * PER : (cc + 1) * PER, :],
                in_=h_banks[c][:].rearrange("p t (v d) -> p d v t", d=D)[:, rows],
                func=ACT.Relu,
            )

        def parity_rows(c):
            half, cc = divmod(c, 2)
            return h_bf[half][:].rearrange("p (f e) v t -> p e f v t", e=2)[:, :, :, cc * PER : (cc + 1) * PER, :]

        def round_even(c):
            nc.gpsimd.tensor_scalar(
                out=parity_rows(c)[:, 0],
                in0=even[c][:].rearrange("p (v f) t -> p f v t", f=2),
                scalar1=1.0,
                scalar2=0.0,
                op0=ALU.mult,
                op1=ALU.add,
            )

        def round_odd(c):
            odd = h_banks[c][:].rearrange("p t (v f e) -> p e f v t", f=2, e=2)[:, 1]
            nc.scalar.activation(out=parity_rows(c)[:, 1], in_=odd, func=ACT.Relu)

        def pool(half):
            by_cloud = pairs[half][:].rearrange("p (v f) t -> p f v t", f=2)
            nc.vector.tensor_tensor(out=z_bf[half][:], in0=by_cloud[:, 0], in1=by_cloud[:, 1], op=ALU.add)

        def quantise_h(half, rows):
            values = h_bf[half][:, rows].rearrange("p d v t -> p (d v t)")
            return quantise("h%d_%d" % (half, rows.start), values, (rows.stop - rows.start) * CLOUDS)

        def quantise_z(half):
            z_codes = sb("z_codes%d" % half, [P, 2 * CLOUDS], U32)
            z_scales = sb("z_scales%d" % half, [P, 2 * CLOUDS], U8)
            for e in range(2):
                cl = slice(e * CLOUDS, (e + 1) * CLOUDS)
                nc.vector.quantize_mx(
                    out=z_codes[:, cl].bitcast(FP8X4),
                    scales=z_scales[:, cl],
                    in_=z_bf[half][:].rearrange("p v t -> p (v t)"),
                )
            return z_codes, z_scales

        accs = [[psum.tile([P, HALF], F32, name="acc%d_%d" % (half, m)) for m in range(M_TILES)] for half in range(HALVES)]

        def product(acc, weights, m, values, start, stop):
            mc = slice(m * P, (m + 1) * P)
            nc.tensor.matmul_mx(
                out=acc,
                lhsT=weights[0][:, mc].bitcast(FP8X4),
                lhsT_scale=weights[1][:, mc],
                rhs=values[0][:].bitcast(FP8X4),
                rhs_scale=values[1][:],
                start=start,
                stop=stop,
            )

        def pooled_product(half, z_q, columns, start, stop):
            for m in range(M_TILES):
                for e in columns:
                    product(accs[half][m][:, e * P : (e + 1) * P], w3_q, m, z_q, start and e == columns[0], stop and e == columns[-1])

        def own_product(half, rows, h_q, start, stop):
            for m in range(M_TILES):
                product(accs[half][m][:, rows.start * CLOUDS : rows.stop * CLOUDS], w2_q, m, h_q, start, stop)

        def leave(half, m, on_vector):
            result = sb("result%d_%d" % (half, m), [P, CLOUDS, D], F32)
            ordered = accs[half][m][:].rearrange("p (d v) -> p v d", d=D)
            if on_vector:
                nc.vector.tensor_scalar(out=result[:], in0=ordered, scalar1=0.0, scalar2=None, op0=ALU.max)
            else:
                nc.scalar.activation(out=result[:], in_=ordered, func=ACT.Relu)
            nc.sync.dma_start(
                out=out[m * P : (m + 1) * P, half * HALF : (half + 1) * HALF],
                in_=result[:].rearrange("p v d -> p (v d)"),
            )

        all_rows, low_rows, high_rows = slice(0, D), slice(0, D // 2), slice(D // 2, D)

        for o in range(PASSES):
            for half in range(HALVES):
                picked = gather(sb("picked%d_%d" % (o, half), [P, HALF], U32), o, half * HALF, HALF)
                for cc in range(2):
                    first_product(2 * half + cc, o, picked[:, cc * CHUNK : (cc + 1) * CHUNK], o == 0, o == PASSES - 1)

        w3_bf, dst, src = group_views(sb("w3_bf", [P, N * PACK], BF16), w3_raw)
        nc.vector.tensor_scalar(out=dst, in0=src, scalar1=1.0 / D, scalar2=None, op0=ALU.mult)
        for c in range(BANKS):
            read_even(c)
        for c in range(BANKS - 1):
            add_odd(c)
        for c in range(2):
            round_even(c)
            round_odd(c)
        idle_bank = psum.tile([P, M_TILES, HALF], F32, name="idle_bank", tag="h_bank0")
        for m in range(M_TILES):
            product(idle_bank[:, m, :], w1_q[0][0], m, w1_q[0][0], True, True)
        pool(0)
        w3_q = quantise("w3", w3_bf[:], N, 0)
        pooled_product(0, quantise_z(0), (0, 1), True, False)
        add_odd(BANKS - 1)
        w2_bf, dst, src = group_views(staged("w2_bf", [P, N * PACK], BF16, 768), w2_raw)
        nc.scalar.activation(out=dst[:, W2_ON_VECTOR:], in_=src[:, W2_ON_VECTOR:], func=ACT.Copy)
        nc.vector.tensor_copy(out=dst[:, 0:W2_ON_VECTOR], in_=src[:, 0:W2_ON_VECTOR])
        round_h(2, all_rows)
        round_h(3, low_rows)
        round_h(3, high_rows)
        h_q0 = quantise_h(0, all_rows)
        w2_q = quantise("w2", w2_bf[:], N)
        own_product(0, all_rows, h_q0, False, True)
        pool(1)
        own_product(1, low_rows, quantise_h(1, low_rows), True, False)
        z_q1 = quantise_z(1)
        h_q1 = quantise_h(1, high_rows)
        for m in range(M_TILES):
            for e in range(2):
                product(accs[1][m][:, e * P : (e + 1) * P], w3_q, m, z_q1, False, False)
            product(accs[1][m][:, P : 2 * P], w2_q, m, h_q1, False, True)
        leave(0, 0, False)
        leave(0, 1, True)
        leave(1, 0, False)
        leave(1, 1, True)
